import numpy as np
import ml_dtypes


def mxq(x, axis, fmt="e4m3"):
    dtype, down = {"e4m3": (ml_dtypes.float8_e4m3fn, 7), "e5m2": (ml_dtypes.float8_e5m2, 14)}[fmt]
    v = np.moveaxis(np.asarray(x, np.float32).astype(ml_dtypes.bfloat16).astype(np.float64), axis, -1)
    blocks = v.reshape(v.shape[:-1] + (-1, 32))
    amax = np.abs(blocks).max(-1, keepdims=True)
    byte = np.maximum(np.where(amax > 0, np.frexp(amax)[1] - 1 + 127, 0) - down, 1)
    scale = np.exp2(byte - 127.0)
    codes = (blocks / scale).astype(np.float32).astype(dtype).astype(np.float64)
    return np.moveaxis((codes * scale).reshape(v.shape), -1, axis)


WIDE = False


def mx_kscale(k):
    if not WIDE:
        return np.ones(k)
    levels = np.array([10, -10, 5, -5, 0])
    if k % 512:
        return np.exp2(np.random.permutation(np.resize(levels, k // 32))).repeat(32)
    a = np.empty((k // 512, 16))
    for p in range(k // 512):
        a[p, :8] = np.random.permutation(np.resize(levels, 8))
        for g in range(8):
            far = levels[np.abs(levels - a[p, g]) >= 10]
            a[p, g + 8] = far[np.random.randint(len(far))]
    return np.exp2(a.ravel()).repeat(32)


def f64(x):
    return np.asarray(x).astype(np.float64)


def striped(idx):
    return np.tile(idx.reshape(-1, 16).T, (8, 1)).astype(np.uint16)


def unstriped(offs):
    return offs[:16].T.reshape(-1).astype(np.int64)


K, T, E, C, N = 512, 768, 24, 128, 128
TOP = 4


def by_expert(wq, xq):
    return np.concatenate([wq[e].T @ xq[:, e * C:(e + 1) * C] for e in range(E)], axis=1)


def setup_inputs():
    n = np.random.standard_normal
    s = mx_kscale(K)[:, None]
    deal = np.repeat(np.arange(E), C).reshape(TOP, T)[:, np.random.permutation(T)]
    deal = np.take_along_axis(deal, np.argsort(np.random.rand(TOP, T), axis=0), axis=0)
    for _ in range(8):
        s_, t_ = np.random.permutation(T).reshape(2, -1); r = np.random.randint(TOP, size=T // 2); x, y = deal[r, s_].copy(), deal[r, t_].copy()
        ok = ~((deal[:, s_] == y).any(0) | (deal[:, t_] == x).any(0)); deal[r[ok], s_[ok]] = y[ok]; deal[r[ok], t_[ok]] = x[ok]
    order = np.lexsort((np.random.rand(TOP * T), deal.reshape(-1)))
    slot_token = order % T; pos = np.empty(TOP * T, np.int64); pos[order] = np.arange(TOP * T); pos = pos.reshape(TOP, T)
    g = np.random.uniform(0.5, 1.5, (TOP, T)); g = g / g.sum(0)
    return {
        "xT": (n((K, T)) * s).astype(np.float32),
        "w": (n((E + 1, K, N)) / np.sqrt(K) / s[None]).astype(np.float32),
        "gate": np.stack([np.tile(r, (N, 1)) for r in g]).astype(np.float32),
        "offs": striped(slot_token),
        "pos1": striped(pos[0]),
        "pos2": striped(pos[1]),
        "pos3": striped(pos[2]),
        "pos4": striped(pos[3]),
    }


def reference(xT, w, gate, offs, pos1, pos2, pos3, pos4):
    idx = unstriped(offs)
    wq = mxq(f64(w), 1, "e4m3")
    xs = mxq(f64(xT), 0, "e4m3")
    ys = wq[E].T @ xs
    xq = mxq(f64(xT)[:, idx], 0, "e4m3")
    y = by_expert(wq, xq)
    return ys + sum(f64(gate[r]) * y[:, unstriped(p)] for r, p in enumerate((pos1, pos2, pos3, pos4)))

@@ -1,0 +1,180 @@
+from contextlib import ExitStack
+
+import concourse.mybir as mybir
+from concourse.masks import make_identity
+
+K, T, E, C, N = 512, 768, 24, 128, 128
+TOP = 4
+SLOTS = E * C
+FLOPS = 2 * K * N * (SLOTS + T)
+
+F32 = mybir.dt.float32
+BF16 = mybir.dt.bfloat16
+U32 = mybir.dt.uint32
+I32 = mybir.dt.int32
+U16 = mybir.dt.uint16
+U8 = mybir.dt.uint8
+FP8X4 = mybir.dt.float8_e4m3fn_x4
+MULT = mybir.AluOpType.mult
+ADD = mybir.AluOpType.add
+
+P = 128
+PACK = 4
+LIST_ROWS = 16
+CHUNK_EXPERTS = 4
+CHUNK = CHUNK_EXPERTS * C
+CHUNKS = E // CHUNK_EXPERTS
+PAIRS = E // 2
+HALF = T // 2
+BLOCKS = T // P
+GATHER_BUFS = 4
+VECTOR_PAIRS = (9, 10, 11)
+
+
+def tile_moe_shr_lin_none_kernel(tc, xT, w, gate, offs, pos1, pos2, pos3, pos4, out):
+    nc = tc.nc
+    with ExitStack() as ctx:
+        keep = ctx.enter_context(tc.tile_pool(name="keep", bufs=1))
+        psum = ctx.enter_context(tc.psum_pool(name="psum", bufs=1))
+
+        x_rows = xT.rearrange("(p h i) t -> p h i t", h=2, i=2)
+        w_rows = w.rearrange("e (p j) n -> p e j n", j=PACK)
+
+        x_low = [keep.tile([P, 2, HALF], F32, name=f"x_low{a}") for a in range(2)]
+        for a in range(2):
+            nc.sync.dma_start(out=x_low[a][:], in_=x_rows[:, 0, :, a * HALF:(a + 1) * HALF])
+        offs_sb = keep.tile([P, SLOTS // LIST_ROWS], U16, name="offs_sb")
+        nc.sync.dma_start(offs_sb[:], offs)
+        w_raw = [keep.tile([P, 2, PACK, N], F32, name=f"w_raw{k}") for k in range(PAIRS)]
+        nc.sync.dma_start(out=w_raw[0][:], in_=w_rows[:, 0:2])
+        x_high = keep.tile([P, 2, T], F32, name="x_high")
+        nc.sync.dma_start(out=x_high[:], in_=x_rows[:, 1])
+        for k in range(1, PAIRS):
+            nc.sync.dma_start(out=w_raw[k][:], in_=w_rows[:, 2 * k:2 * k + 2])
+        ws_raw = keep.tile([P, 1, PACK, N], F32, name="ws_raw")
+        nc.sync.dma_start(out=ws_raw[:], in_=w_rows[:, E:E + 1])
+        pos_sb = []
+        for r, pos in enumerate((pos1, pos2, pos3, pos4)):
+            pos_tile = keep.tile([P, T // LIST_ROWS], U16, name=f"pos_sb{r}")
+            nc.sync.dma_start(pos_tile[:], pos)
+            pos_sb.append(pos_tile)
+        gate_sb = keep.tile([P, TOP, T], F32, name="gate_sb")
+        nc.sync.dma_start(out=gate_sb[:], in_=gate.rearrange("r n t -> n r t"))
+
+        ident = keep.tile([P, P], F32, name="ident")
+        make_identity(nc, ident[:])
+
+        pairs = keep.tile([P, 2 * T], U32, name="pairs", align_bytes=64)
+
+        def pair_view(h, t0, t1):
+            return pairs[:, h * T + t0:h * T + t1].bitcast(BF16).rearrange("p (t i) -> p t i", i=2)
+
+        nc.scalar.copy(out=pair_view(0, 0, HALF), in_=x_low[0][:].rearrange("p i t -> p t i"))
+        nc.vector.tensor_copy(out=pair_view(0, HALF, T), in_=x_low[1][:].rearrange("p i t -> p t i"))
+
+        gathered = [keep.tile([P, 2, CHUNK], U32, name=f"gathered{c}", tag=f"gathered{c % GATHER_BUFS}", align_bytes=64) for c in range(GATHER_BUFS)]
+        x_bf = [keep.tile([P, CHUNK * PACK], BF16, name=f"x_bf{c}", align_bytes=64) for c in range(CHUNKS)]
+        w_bf = [keep.tile([P, CHUNK * PACK], BF16, name=f"w_bf{c}", align_bytes=64) for c in range(CHUNKS)]
+        x_codes = [keep.tile([P, CHUNK], U32, name=f"x_codes{c}", align_bytes=64) for c in range(CHUNKS)]
+        w_codes = [keep.tile([P, CHUNK], U32, name=f"w_codes{c}", align_bytes=64) for c in range(CHUNKS)]
+        x_scales = [keep.tile([P, CHUNK], U8, name=f"x_scales{c}", align_bytes=64) for c in range(CHUNKS)]
+        w_scales = [keep.tile([P, CHUNK], U8, name=f"w_scales{c}", align_bytes=64) for c in range(CHUNKS)]
+        y_bank = [psum.tile([P, CHUNK], F32, name=f"y_bank{c}", tag=f"bank{c}") for c in range(CHUNKS)]
+        y = keep.tile([P, SLOTS], F32, name="y")
+
+        def gather(c, h):
+            cols = slice(c * CHUNK // LIST_ROWS, (c + 1) * CHUNK // LIST_ROWS)
+            nc.vector.tensor_copy(out=gathered[c][:, h, :], in_=pairs[:, h * T:(h + 1) * T].indirect(offs_sb[:, cols]))
+
+        def weave(c):
+            nc.scalar.copy(out=x_bf[c][:].bitcast(U32).rearrange("p (s h) -> p s h", h=2),
+                           in_=gathered[c][:].rearrange("p h s -> p s h"))
+
+        def interleave(copy, dst, src):
+            copy(out=dst.rearrange("p (e g i j) -> p e g j i", g=N // 4, i=4, j=PACK),
+                 in_=src.rearrange("p e j (g i) -> p e g j i", i=4))
+
+        def round_weights(k):
+            copy = nc.vector.tensor_copy if k in VECTOR_PAIRS else nc.scalar.copy
+            width = 2 * N * PACK
+            interleave(copy, w_bf[k // 2][:, (k % 2) * width:(k % 2 + 1) * width], w_raw[k][:])
+
+        def quantise(codes, scales, values):
+            nc.vector.quantize_mx(out=codes.bitcast(FP8X4), scales=scales, in_=values)
+
+        def multiply(c):
+            for e in range(CHUNK_EXPERTS):
+                cols = slice(e * C, (e + 1) * C)
+                nc.tensor.matmul_mx(out=y_bank[c][:, cols], lhsT=w_codes[c][:, cols].bitcast(FP8X4), lhsT_scale=w_scales[c][:, cols],
+                                    rhs=x_codes[c][:, cols].bitcast(FP8X4), rhs_scale=x_scales[c][:, cols], start=True, stop=True)
+
+        def evacuate(c):
+            nc.scalar.copy(out=y[:, c * CHUNK:(c + 1) * CHUNK], in_=y_bank[c][:])
+
+        round_weights(0)
+        nc.scalar.copy(out=pair_view(1, 0, T), in_=x_high[:].rearrange("p i t -> p t i"))
+        round_weights(1)
+        for c in range(CHUNKS):
+            if c >= GATHER_BUFS:
+                gathered.append(keep.tile([P, 2, CHUNK], U32, name=f"gathered{c}", tag=f"gathered{c % GATHER_BUFS}", align_bytes=64))
+            gather(c, 0)
+            gather(c, 1)
+            if c + 1 < CHUNKS:
+                round_weights(2 * c + 2)
+            if c >= 1:
+                evacuate(c - 1)
+            weave(c)
+            quantise(w_codes[c][:], w_scales[c][:], w_bf[c][:])
+            quantise(x_codes[c][:], x_scales[c][:], x_bf[c][:])
+            if c + 1 < CHUNKS:
+                round_weights(2 * c + 3)
+            multiply(c)
+        evacuate(CHUNKS - 1)
+
+        xs_bf = keep.tile([P, T * PACK], BF16, name="xs_bf", tag=f"gathered{(CHUNKS - 1) % GATHER_BUFS}", align_bytes=64)
+        nc.vector.tensor_copy(out=xs_bf[:].bitcast(I32).rearrange("p (t h) -> p t h", h=2),
+                              in_=pairs[:].bitcast(I32).rearrange("p (h t) -> p t h", h=2))
+        ws_bf = keep.tile([P, N * PACK], BF16, name="ws_bf", align_bytes=64)
+        interleave(nc.scalar.copy, ws_bf[:], ws_raw[:])
+        ws_codes = keep.tile([P, N], U32, name="ws_codes", align_bytes=64)
+        ws_scales = keep.tile([P, N], U8, name="ws_scales", align_bytes=64)
+        xs_codes = keep.tile([P, T], U32, name="xs_codes", align_bytes=64)
+        xs_scales = keep.tile([P, T], U8, name="xs_scales", align_bytes=64)
+        quantise(ws_codes[:], ws_scales[:], ws_bf[:])
+        ys = keep.tile([P, T], F32, name="ys")
+        for b, (t0, t1) in enumerate(((0, 512), (512, T))):
+            quantise(xs_codes[:, t0:t1], xs_scales[:, t0:t1], xs_bf[:, t0 * PACK:t1 * PACK])
+            ys_bank = psum.tile([P, t1 - t0], F32, name=f"ys_bank{b}", tag=f"bank{CHUNKS + b}")
+            nc.tensor.matmul_mx(out=ys_bank[:], lhsT=ws_codes[:].bitcast(FP8X4), lhsT_scale=ws_scales[:],
+                                rhs=xs_codes[:, t0:t1].bitcast(FP8X4), rhs_scale=xs_scales[:, t0:t1], start=True, stop=True)
+            nc.scalar.copy(out=ys[:, t0:t1], in_=ys_bank[:])
+
+        gated = [[keep.tile([P, HALF], F32, name=f"gated{r}_{a}") for a in range(2)] for r in range(TOP)]
+
+        def fetch(r, a):
+            cols = slice(a * HALF // LIST_ROWS, (a + 1) * HALF // LIST_ROWS)
+            nc.vector.tensor_tensor(gated[r][a][:], y[:].indirect(pos_sb[r][:, cols]), gate_sb[:, r, a * HALF:(a + 1) * HALF], MULT)
+
+        turned = [psum.tile([P, P], F32, name=f"turned{b}", tag=f"bank{b}") for b in range(BLOCKS)]
+        per_half = BLOCKS // 2
+        for b in range(BLOCKS):
+            nc.tensor.matmul(turned[b][:], ys[:, b * P:(b + 1) * P], ident[:], start=True, stop=False, is_transpose=True)
+        partial = []
+        for a in range(2):
+            for r in range(TOP - 1):
+                fetch(r, a)
+                for i in range(per_half):
+                    nc.tensor.matmul(turned[a * per_half + i][:], gated[r][a][:, i * P:(i + 1) * P], ident[:],
+                                     start=False, stop=(r == TOP - 2), is_transpose=True)
+            back = psum.tile([P, HALF], F32, name=f"back{a}", tag=f"bank{CHUNKS + a}")
+            for i in range(per_half):
+                turned_sb = keep.tile([P, P], F32, name=f"turned_sb{a}_{i}")
+                nc.scalar.copy(out=turned_sb[:], in_=turned[a * per_half + i][:])
+                nc.tensor.transpose(back[:, i * P:(i + 1) * P], turned_sb[:], ident[:])
+            partial.append(back)
+        for a in range(2):
+            fetch(TOP - 1, a)
+        for a in range(2):
+            result = keep.tile([P, HALF], F32, name=f"result{a}")
+            nc.vector.tensor_tensor(result[:], partial[a][:], gated[TOP - 1][a][:], ADD)
+            nc.sync.dma_start(out=out[:, a * HALF:(a + 1) * HALF], in_=result[:])

@@ -27,8 +27,8 @@ CHUNKS = E // CHUNK_EXPERTS
 PAIRS = E // 2
 HALF = T // 2
 BLOCKS = T // P
-GATHER_BUFS = 4
-VECTOR_PAIRS = (9, 10, 11)
+AHEAD = 4
+GPSIMD_PAIRS = range(3, 8)
 
 
 def tile_moe_shr_lin_none_kernel(tc, xT, w, gate, offs, pos1, pos2, pos3, pos4, out):
@@ -45,10 +45,11 @@ def tile_moe_shr_lin_none_kernel(tc, xT, w, gate, offs, pos1, pos2, pos3, pos4, 
             nc.sync.dma_start(out=x_low[a][:], in_=x_rows[:, 0, :, a * HALF:(a + 1) * HALF])
         offs_sb = keep.tile([P, SLOTS // LIST_ROWS], U16, name="offs_sb")
         nc.sync.dma_start(offs_sb[:], offs)
-        w_raw = [keep.tile([P, 2, PACK, N], F32, name=f"w_raw{k}") for k in range(PAIRS)]
+        w_raw = [keep.tile([P, 2, PACK, N], F32, name=f"w_raw{k}", tag=f"w_raw{k}") for k in range(PAIRS)]
         nc.sync.dma_start(out=w_raw[0][:], in_=w_rows[:, 0:2])
-        x_high = keep.tile([P, 2, T], F32, name="x_high")
-        nc.sync.dma_start(out=x_high[:], in_=x_rows[:, 1])
+        x_high = [keep.tile([P, 2, HALF], F32, name=f"x_high{a}", tag=f"late{a}", align_bytes=64) for a in range(2)]
+        for a in range(2):
+            nc.sync.dma_start(out=x_high[a][:], in_=x_rows[:, 1, :, a * HALF:(a + 1) * HALF])
         for k in range(1, PAIRS):
             nc.sync.dma_start(out=w_raw[k][:], in_=w_rows[:, 2 * k:2 * k + 2])
         ws_raw = keep.tile([P, 1, PACK, N], F32, name="ws_raw")
@@ -72,15 +73,14 @@ def tile_moe_shr_lin_none_kernel(tc, xT, w, gate, offs, pos1, pos2, pos3, pos4, 
         nc.scalar.copy(out=pair_view(0, 0, HALF), in_=x_low[0][:].rearrange("p i t -> p t i"))
         nc.vector.tensor_copy(out=pair_view(0, HALF, T), in_=x_low[1][:].rearrange("p i t -> p t i"))
 
-        gathered = [keep.tile([P, 2, CHUNK], U32, name=f"gathered{c}", tag=f"gathered{c % GATHER_BUFS}", align_bytes=64) for c in range(GATHER_BUFS)]
+        gathered = [keep.tile([P, 2, CHUNK], U32, name=f"gathered{c}", align_bytes=64) for c in range(AHEAD)]
         x_bf = [keep.tile([P, CHUNK * PACK], BF16, name=f"x_bf{c}", align_bytes=64) for c in range(CHUNKS)]
-        w_bf = [keep.tile([P, CHUNK * PACK], BF16, name=f"w_bf{c}", align_bytes=64) for c in range(CHUNKS)]
+        w_bf = [keep.tile([P, CHUNK * PACK], BF16, name=f"w_bf{c}", tag=f"w_bf{c}", align_bytes=64) for c in range(CHUNKS)]
         x_codes = [keep.tile([P, CHUNK], U32, name=f"x_codes{c}", align_bytes=64) for c in range(CHUNKS)]
         w_codes = [keep.tile([P, CHUNK], U32, name=f"w_codes{c}", align_bytes=64) for c in range(CHUNKS)]
         x_scales = [keep.tile([P, CHUNK], U8, name=f"x_scales{c}", align_bytes=64) for c in range(CHUNKS)]
         w_scales = [keep.tile([P, CHUNK], U8, name=f"w_scales{c}", align_bytes=64) for c in range(CHUNKS)]
         y_bank = [psum.tile([P, CHUNK], F32, name=f"y_bank{c}", tag=f"bank{c}") for c in range(CHUNKS)]
-        y = keep.tile([P, SLOTS], F32, name="y")
 
         def gather(c, h):
             cols = slice(c * CHUNK // LIST_ROWS, (c + 1) * CHUNK // LIST_ROWS)
@@ -95,9 +95,13 @@ def tile_moe_shr_lin_none_kernel(tc, xT, w, gate, offs, pos1, pos2, pos3, pos4, 
                  in_=src.rearrange("p e j (g i) -> p e g j i", i=4))
 
         def round_weights(k):
-            copy = nc.vector.tensor_copy if k in VECTOR_PAIRS else nc.scalar.copy
             width = 2 * N * PACK
-            interleave(copy, w_bf[k // 2][:, (k % 2) * width:(k % 2 + 1) * width], w_raw[k][:])
+            dst = w_bf[k // 2][:, (k % 2) * width:(k % 2 + 1) * width]
+            if k in GPSIMD_PAIRS:
+                nc.gpsimd.tensor_scalar(out=dst.rearrange("p (e n j) -> p e n j", n=N, j=PACK), in0=w_raw[k][:].rearrange("p e j n -> p e n j"),
+                                        scalar1=1.0, scalar2=0.0, op0=MULT, op1=ADD)
+            else:
+                interleave(nc.scalar.copy, dst, w_raw[k][:])
 
         def quantise(codes, scales, values):
             nc.vector.quantize_mx(out=codes.bitcast(FP8X4), scales=scales, in_=values)
@@ -112,26 +116,30 @@ def tile_moe_shr_lin_none_kernel(tc, xT, w, gate, offs, pos1, pos2, pos3, pos4, 
             nc.scalar.copy(out=y[:, c * CHUNK:(c + 1) * CHUNK], in_=y_bank[c][:])
 
         round_weights(0)
-        nc.scalar.copy(out=pair_view(1, 0, T), in_=x_high[:].rearrange("p i t -> p t i"))
-        round_weights(1)
+        for a in range(2):
+            nc.scalar.copy(out=pair_view(1, a * HALF, (a + 1) * HALF), in_=x_high[a][:].rearrange("p i t -> p t i"))
+        for c in range(AHEAD, CHUNKS):
+            gathered.append(keep.tile([P, 2, CHUNK], U32, name=f"gathered{c}", tag=f"late{c - AHEAD}", align_bytes=64))
         for c in range(CHUNKS):
-            if c >= GATHER_BUFS:
-                gathered.append(keep.tile([P, 2, CHUNK], U32, name=f"gathered{c}", tag=f"gathered{c % GATHER_BUFS}", align_bytes=64))
             gather(c, 0)
             gather(c, 1)
-            if c + 1 < CHUNKS:
-                round_weights(2 * c + 2)
-            if c >= 1:
-                evacuate(c - 1)
+        for k in range(1, 8):
+            round_weights(k)
+        for c in range(AHEAD):
             weave(c)
+        for c in range(AHEAD, CHUNKS):
+            round_weights(c + 4)
+            weave(c)
+        for k in range(10, PAIRS):
+            round_weights(k)
+        y = keep.tile([P, SLOTS], F32, name="y", tag=f"w_raw{PAIRS - 1}")
+        for c in range(CHUNKS):
             quantise(w_codes[c][:], w_scales[c][:], w_bf[c][:])
             quantise(x_codes[c][:], x_scales[c][:], x_bf[c][:])
-            if c + 1 < CHUNKS:
-                round_weights(2 * c + 3)
             multiply(c)
-        evacuate(CHUNKS - 1)
+            evacuate(c)
 
-        xs_bf = keep.tile([P, T * PACK], BF16, name="xs_bf", tag=f"gathered{(CHUNKS - 1) % GATHER_BUFS}", align_bytes=64)
+        xs_bf = keep.tile([P, T * PACK], BF16, name="xs_bf", tag=f"w_bf{CHUNKS - 1}", align_bytes=64)
         nc.vector.tensor_copy(out=xs_bf[:].bitcast(I32).rearrange("p (t h) -> p t h", h=2),
                               in_=pairs[:].bitcast(I32).rearrange("p (h t) -> p t h", h=2))
         ws_bf = keep.tile([P, N * PACK], BF16, name="ws_bf", align_bytes=64)

from contextlib import ExitStack

import concourse.mybir as mybir
from concourse.masks import make_identity

K, T, E, C, N = 512, 768, 24, 128, 128
TOP = 4
SLOTS = E * C
FLOPS = 2 * K * N * (SLOTS + T)

F32 = mybir.dt.float32
BF16 = mybir.dt.bfloat16
U32 = mybir.dt.uint32
I32 = mybir.dt.int32
U16 = mybir.dt.uint16
U8 = mybir.dt.uint8
FP8X4 = mybir.dt.float8_e4m3fn_x4
MULT = mybir.AluOpType.mult
ADD = mybir.AluOpType.add

P = 128
PACK = 4
LIST_ROWS = 16
CHUNK_EXPERTS = 4
CHUNK = CHUNK_EXPERTS * C
CHUNKS = E // CHUNK_EXPERTS
PAIRS = E // 2
HALF = T // 2
BLOCKS = T // P
AHEAD = 4
GPSIMD_PAIRS = range(3, 8)


def tile_moe_shr_lin_none_kernel(tc, xT, w, gate, offs, pos1, pos2, pos3, pos4, out):
    nc = tc.nc
    with ExitStack() as ctx:
        keep = ctx.enter_context(tc.tile_pool(name="keep", bufs=1))
        psum = ctx.enter_context(tc.psum_pool(name="psum", bufs=1))

        x_rows = xT.rearrange("(p h i) t -> p h i t", h=2, i=2)
        w_rows = w.rearrange("e (p j) n -> p e j n", j=PACK)

        x_low = [keep.tile([P, 2, HALF], F32, name=f"x_low{a}") for a in range(2)]
        for a in range(2):
            nc.sync.dma_start(out=x_low[a][:], in_=x_rows[:, 0, :, a * HALF:(a + 1) * HALF])
        offs_sb = keep.tile([P, SLOTS // LIST_ROWS], U16, name="offs_sb")
        nc.sync.dma_start(offs_sb[:], offs)
        w_raw = [keep.tile([P, 2, PACK, N], F32, name=f"w_raw{k}", tag=f"w_raw{k}") for k in range(PAIRS)]
        nc.sync.dma_start(out=w_raw[0][:], in_=w_rows[:, 0:2])
        x_high = [keep.tile([P, 2, HALF], F32, name=f"x_high{a}", tag=f"late{a}", align_bytes=64) for a in range(2)]
        for a in range(2):
            nc.sync.dma_start(out=x_high[a][:], in_=x_rows[:, 1, :, a * HALF:(a + 1) * HALF])
        for k in range(1, PAIRS):
            nc.sync.dma_start(out=w_raw[k][:], in_=w_rows[:, 2 * k:2 * k + 2])
        ws_raw = keep.tile([P, 1, PACK, N], F32, name="ws_raw")
        nc.sync.dma_start(out=ws_raw[:], in_=w_rows[:, E:E + 1])
        pos_sb = []
        for r, pos in enumerate((pos1, pos2, pos3, pos4)):
            pos_tile = keep.tile([P, T // LIST_ROWS], U16, name=f"pos_sb{r}")
            nc.sync.dma_start(pos_tile[:], pos)
            pos_sb.append(pos_tile)
        gate_sb = keep.tile([P, TOP, T], F32, name="gate_sb")
        nc.sync.dma_start(out=gate_sb[:], in_=gate.rearrange("r n t -> n r t"))

        ident = keep.tile([P, P], F32, name="ident")
        make_identity(nc, ident[:])

        pairs = keep.tile([P, 2 * T], U32, name="pairs", align_bytes=64)

        def pair_view(h, t0, t1):
            return pairs[:, h * T + t0:h * T + t1].bitcast(BF16).rearrange("p (t i) -> p t i", i=2)

        nc.scalar.copy(out=pair_view(0, 0, HALF), in_=x_low[0][:].rearrange("p i t -> p t i"))
        nc.vector.tensor_copy(out=pair_view(0, HALF, T), in_=x_low[1][:].rearrange("p i t -> p t i"))

        gathered = [keep.tile([P, 2, CHUNK], U32, name=f"gathered{c}", align_bytes=64) for c in range(AHEAD)]
        x_bf = [keep.tile([P, CHUNK * PACK], BF16, name=f"x_bf{c}", align_bytes=64) for c in range(CHUNKS)]
        w_bf = [keep.tile([P, CHUNK * PACK], BF16, name=f"w_bf{c}", tag=f"w_bf{c}", align_bytes=64) for c in range(CHUNKS)]
        x_codes = [keep.tile([P, CHUNK], U32, name=f"x_codes{c}", align_bytes=64) for c in range(CHUNKS)]
        w_codes = [keep.tile([P, CHUNK], U32, name=f"w_codes{c}", align_bytes=64) for c in range(CHUNKS)]
        x_scales = [keep.tile([P, CHUNK], U8, name=f"x_scales{c}", align_bytes=64) for c in range(CHUNKS)]
        w_scales = [keep.tile([P, CHUNK], U8, name=f"w_scales{c}", align_bytes=64) for c in range(CHUNKS)]
        y_bank = [psum.tile([P, CHUNK], F32, name=f"y_bank{c}", tag=f"bank{c}") for c in range(CHUNKS)]

        def gather(c, h):
            cols = slice(c * CHUNK // LIST_ROWS, (c + 1) * CHUNK // LIST_ROWS)
            nc.vector.tensor_copy(out=gathered[c][:, h, :], in_=pairs[:, h * T:(h + 1) * T].indirect(offs_sb[:, cols]))

        def weave(c):
            nc.scalar.copy(out=x_bf[c][:].bitcast(U32).rearrange("p (s h) -> p s h", h=2),
                           in_=gathered[c][:].rearrange("p h s -> p s h"))

        def interleave(copy, dst, src):
            copy(out=dst.rearrange("p (e g i j) -> p e g j i", g=N // 4, i=4, j=PACK),
                 in_=src.rearrange("p e j (g i) -> p e g j i", i=4))

        def round_weights(k):
            width = 2 * N * PACK
            dst = w_bf[k // 2][:, (k % 2) * width:(k % 2 + 1) * width]
            if k in GPSIMD_PAIRS:
                nc.gpsimd.tensor_scalar(out=dst.rearrange("p (e n j) -> p e n j", n=N, j=PACK), in0=w_raw[k][:].rearrange("p e j n -> p e n j"),
                                        scalar1=1.0, scalar2=0.0, op0=MULT, op1=ADD)
            else:
                interleave(nc.scalar.copy, dst, w_raw[k][:])

        def quantise(codes, scales, values):
            nc.vector.quantize_mx(out=codes.bitcast(FP8X4), scales=scales, in_=values)

        def multiply(c):
            for e in range(CHUNK_EXPERTS):
                cols = slice(e * C, (e + 1) * C)
                nc.tensor.matmul_mx(out=y_bank[c][:, cols], lhsT=w_codes[c][:, cols].bitcast(FP8X4), lhsT_scale=w_scales[c][:, cols],
                                    rhs=x_codes[c][:, cols].bitcast(FP8X4), rhs_scale=x_scales[c][:, cols], start=True, stop=True)

        def evacuate(c):
            nc.scalar.copy(out=y[:, c * CHUNK:(c + 1) * CHUNK], in_=y_bank[c][:])

        round_weights(0)
        for a in range(2):
            nc.scalar.copy(out=pair_view(1, a * HALF, (a + 1) * HALF), in_=x_high[a][:].rearrange("p i t -> p t i"))
        for c in range(AHEAD, CHUNKS):
            gathered.append(keep.tile([P, 2, CHUNK], U32, name=f"gathered{c}", tag=f"late{c - AHEAD}", align_bytes=64))
        for c in range(CHUNKS):
            gather(c, 0)
            gather(c, 1)
        for k in range(1, 8):
            round_weights(k)
        for c in range(AHEAD):
            weave(c)
        for c in range(AHEAD, CHUNKS):
            round_weights(c + 4)
            weave(c)
        for k in range(10, PAIRS):
            round_weights(k)
        y = keep.tile([P, SLOTS], F32, name="y", tag=f"w_raw{PAIRS - 1}")
        for c in range(CHUNKS):
            quantise(w_codes[c][:], w_scales[c][:], w_bf[c][:])
            quantise(x_codes[c][:], x_scales[c][:], x_bf[c][:])
            multiply(c)
            evacuate(c)

        xs_bf = keep.tile([P, T * PACK], BF16, name="xs_bf", tag=f"w_bf{CHUNKS - 1}", align_bytes=64)
        nc.vector.tensor_copy(out=xs_bf[:].bitcast(I32).rearrange("p (t h) -> p t h", h=2),
                              in_=pairs[:].bitcast(I32).rearrange("p (h t) -> p t h", h=2))
        ws_bf = keep.tile([P, N * PACK], BF16, name="ws_bf", align_bytes=64)
        interleave(nc.scalar.copy, ws_bf[:], ws_raw[:])
        ws_codes = keep.tile([P, N], U32, name="ws_codes", align_bytes=64)
        ws_scales = keep.tile([P, N], U8, name="ws_scales", align_bytes=64)
        xs_codes = keep.tile([P, T], U32, name="xs_codes", align_bytes=64)
        xs_scales = keep.tile([P, T], U8, name="xs_scales", align_bytes=64)
        quantise(ws_codes[:], ws_scales[:], ws_bf[:])
        ys = keep.tile([P, T], F32, name="ys")
        for b, (t0, t1) in enumerate(((0, 512), (512, T))):
            quantise(xs_codes[:, t0:t1], xs_scales[:, t0:t1], xs_bf[:, t0 * PACK:t1 * PACK])
            ys_bank = psum.tile([P, t1 - t0], F32, name=f"ys_bank{b}", tag=f"bank{CHUNKS + b}")
            nc.tensor.matmul_mx(out=ys_bank[:], lhsT=ws_codes[:].bitcast(FP8X4), lhsT_scale=ws_scales[:],
                                rhs=xs_codes[:, t0:t1].bitcast(FP8X4), rhs_scale=xs_scales[:, t0:t1], start=True, stop=True)
            nc.scalar.copy(out=ys[:, t0:t1], in_=ys_bank[:])

        gated = [[keep.tile([P, HALF], F32, name=f"gated{r}_{a}") for a in range(2)] for r in range(TOP)]

        def fetch(r, a):
            cols = slice(a * HALF // LIST_ROWS, (a + 1) * HALF // LIST_ROWS)
            nc.vector.tensor_tensor(gated[r][a][:], y[:].indirect(pos_sb[r][:, cols]), gate_sb[:, r, a * HALF:(a + 1) * HALF], MULT)

        turned = [psum.tile([P, P], F32, name=f"turned{b}", tag=f"bank{b}") for b in range(BLOCKS)]
        per_half = BLOCKS // 2
        for b in range(BLOCKS):
            nc.tensor.matmul(turned[b][:], ys[:, b * P:(b + 1) * P], ident[:], start=True, stop=False, is_transpose=True)
        partial = []
        for a in range(2):
            for r in range(TOP - 1):
                fetch(r, a)
                for i in range(per_half):
                    nc.tensor.matmul(turned[a * per_half + i][:], gated[r][a][:, i * P:(i + 1) * P], ident[:],
                                     start=False, stop=(r == TOP - 2), is_transpose=True)
            back = psum.tile([P, HALF], F32, name=f"back{a}", tag=f"bank{CHUNKS + a}")
            for i in range(per_half):
                turned_sb = keep.tile([P, P], F32, name=f"turned_sb{a}_{i}")
                nc.scalar.copy(out=turned_sb[:], in_=turned[a * per_half + i][:])
                nc.tensor.transpose(back[:, i * P:(i + 1) * P], turned_sb[:], ident[:])
            partial.append(back)
        for a in range(2):
            fetch(TOP - 1, a)
        for a in range(2):
            result = keep.tile([P, HALF], F32, name=f"result{a}")
            nc.vector.tensor_tensor(result[:], partial[a][:], gated[TOP - 1][a][:], ADD)
            nc.sync.dma_start(out=out[:, a * HALF:(a + 1) * HALF], in_=result[:])
